import numpy as np
import ml_dtypes


def mxq(x, axis, fmt="e4m3"):
    dtype, down = {"e4m3": (ml_dtypes.float8_e4m3fn, 7), "e5m2": (ml_dtypes.float8_e5m2, 14)}[fmt]
    v = np.moveaxis(np.asarray(x, np.float32).astype(ml_dtypes.bfloat16).astype(np.float64), axis, -1)
    blocks = v.reshape(v.shape[:-1] + (-1, 32))
    amax = np.abs(blocks).max(-1, keepdims=True)
    byte = np.maximum(np.where(amax > 0, np.frexp(amax)[1] - 1 + 127, 0) - down, 1)
    scale = np.exp2(byte - 127.0)
    codes = (blocks / scale).astype(np.float32).astype(dtype).astype(np.float64)
    return np.moveaxis((codes * scale).reshape(v.shape), -1, axis)


WIDE = False


def mx_kscale(k):
    if not WIDE:
        return np.ones(k)
    levels = np.array([10, -10, 5, -5, 0])
    if k % 512:
        return np.exp2(np.random.permutation(np.resize(levels, k // 32))).repeat(32)
    a = np.empty((k // 512, 16))
    for p in range(k // 512):
        a[p, :8] = np.random.permutation(np.resize(levels, 8))
        for g in range(8):
            far = levels[np.abs(levels - a[p, g]) >= 10]
            a[p, g + 8] = far[np.random.randint(len(far))]
    return np.exp2(a.ravel()).repeat(32)


def f64(x):
    return np.asarray(x).astype(np.float64)


E2M1 = np.array([0.0, 0.5, 1.0, 1.5, 2.0, 3.0, 4.0, 6.0, -0.0, -0.5, -1.0, -1.5, -2.0, -3.0, -4.0, -6.0])


def pack_weight(w, fmt):
    k, n = w.shape
    w = f64(np.asarray(w, np.float32).astype(ml_dtypes.bfloat16)).reshape(k // 32, 32, n)
    amax = np.abs(w).max(1)
    if fmt == "e4m3":
        byte = np.frexp(amax)[1] - 1 + 127 - 7
    else:
        mant, ex = np.frexp(amax / 6.0)
        byte = np.where(mant > 0.5, ex, ex - 1) + 127
    byte = np.clip(np.where(amax > 0, byte, 1), 1, 254)
    scaled = (w * np.exp2(127.0 - byte)[:, None, :]).reshape(k, n).astype(np.float32)
    by_word = np.ascontiguousarray(scaled.reshape(k // 512, 128, 4, n).transpose(0, 1, 3, 2))
    if fmt == "e4m3":
        words = by_word.astype(ml_dtypes.float8_e4m3fn).view(np.uint8)
    else:
        c = by_word.astype(ml_dtypes.float4_e2m1fn).view(np.uint8) & 0xF
        words = (c[..., 0::2] | (c[..., 1::2] << 4)).reshape(k // 512, 128, 2 * n)
    return np.ascontiguousarray(words), np.ascontiguousarray(byte.astype(np.uint8).reshape(k // 512, 16, n))


def unpack_weight(words, scales, fmt):
    g, _, n = scales.shape
    words = np.ascontiguousarray(words).reshape(g, 128, n, -1)
    if fmt == "e4m3":
        vals = words.view(ml_dtypes.float8_e4m3fn).astype(np.float64)
    else:
        nib = np.empty((g, 128, n, 4), np.uint8)
        nib[..., 0::2] = words & 0xF
        nib[..., 1::2] = words >> 4
        vals = E2M1[nib]
    vals = vals * np.repeat(np.exp2(scales.astype(np.float64) - 127.0), 8, axis=1)[..., None]
    return vals.transpose(0, 1, 3, 2).reshape(g * 512, n)


K, R, M, T = 1536, 512, 1536, 1024


def setup_inputs():
    n = np.random.standard_normal
    s = mx_kscale(K)[:, None]
    u = mx_kscale(R)[:, None]
    p_w4 = pack_weight(n((K, M)) / np.sqrt(K) / s, "e2m1")
    return {
        "x": (n((K, T)) * s).astype(np.float32),
        "w4_words": p_w4[0],
        "w4_scales": p_w4[1],
        "down": (n((K, R)) / np.sqrt(K) / s * u.T).astype(np.float32),
        "up": (0.5 * n((R, M)) / np.sqrt(R) / u).astype(np.float32),
    }


def reference(x, w4_words, w4_scales, down, up):
    x_ = mxq(f64(x), 0, "e4m3")
    w4_ = unpack_weight(w4_words, w4_scales, "e2m1")
    down_ = mxq(f64(down), 0, "e4m3")
    up_ = mxq(f64(up), 0, "e4m3")
    h_ = mxq(down_.T @ x_, 0, "e4m3")
    y = w4_.T @ x_ + up_.T @ h_
    return y

@@ -1,0 +1,239 @@
+from contextlib import ExitStack
+
+import concourse.mybir as mybir
+
+K, R, M, T = 1536, 512, 1536, 1024
+FLOPS = 2 * T * (K * R + K * M + R * M)
+
+F32 = mybir.dt.float32
+BF16 = mybir.dt.bfloat16
+U32 = mybir.dt.uint32
+I32 = mybir.dt.int32
+U8 = mybir.dt.uint8
+FP8X4 = mybir.dt.float8_e4m3fn_x4
+FP4X4 = mybir.dt.float4_e2m1fn_x4
+
+P = 128
+PACK = 4
+W = 512
+HALF = W // 2
+PASSES = K // W
+N_TILES = M // P
+T_HALVES = T // W
+EARLY = 4
+
+
+def tile_mix_lowrank_fm_none_kernel(tc, x, w4_words, w4_scales, down, up, out):
+    nc = tc.nc
+
+    with ExitStack() as ctx:
+        raw = ctx.enter_context(tc.tile_pool(name="raw", bufs=1))
+        stage = ctx.enter_context(tc.tile_pool(name="stage", bufs=4))
+        keep = ctx.enter_context(tc.tile_pool(name="keep", bufs=1))
+        outs = ctx.enter_context(tc.tile_pool(name="outs", bufs=24))
+        psum = ctx.enter_context(tc.psum_pool(name="psum", bufs=8))
+        ctx.enter_context(tc.manual_schedule())
+
+        w_scales = keep.tile([P, PASSES, M], U8, name="w_scales", align_bytes=64)
+        nc.vector.memset(w_scales[:].rearrange("p a n -> p (a n)").bitcast(I32), 0)
+        warm_in = keep.tile([P, 8], F32, name="warm_in")
+        warm_out = keep.tile([P, 8], F32, name="warm_out")
+        nc.vector.memset(warm_in[:], 0.0)
+        nc.scalar.copy(out=warm_out[:], in_=warm_in[:])
+
+        def load_rows(name, rows):
+            tile = raw.tile([P, PACK, rows.shape[1]], F32, name=name)
+            nc.sync.dma_start(out=tile[:], in_=rows.rearrange("(p j) w -> p j w", j=PACK))
+            return tile
+
+        def load_x(h, a):
+            return load_rows(f"x_{h}_{a}", x[a * W:(a + 1) * W, h * W:(h + 1) * W])
+
+        def load_down(a):
+            return load_rows(f"down_{a}", down[a * W:(a + 1) * W, :])
+
+        def load_words(name, lo, hi):
+            tile = keep.tile([P, PASSES, 2 * (hi - lo)], U8, name=name, align_bytes=64)
+            nc.sync.dma_start(
+                out=tile[:].bitcast(I32),
+                in_=w4_words[:, :, 2 * lo:2 * hi].rearrange("a p c -> p a c").bitcast(I32),
+            )
+            return tile
+
+        x_raw = [[None] * PASSES for h in range(T_HALVES)]
+        d_raw = [None] * PASSES
+        x_raw[0][0] = load_x(0, 0)
+        d_raw[0] = load_down(0)
+        w_a = load_words("w_a", 0, EARLY * P)
+        for q in range(4):
+            nc.scalar.dma_start(
+                out=w_scales[32 * q:32 * q + 4, :, :].bitcast(I32),
+                in_=w4_scales[:, 4 * q:4 * q + 4, :].rearrange("a r n -> r a n").bitcast(I32),
+            )
+        x_raw[0][1] = load_x(0, 1)
+        d_raw[1] = load_down(1)
+        x_raw[0][2] = load_x(0, 2)
+        d_raw[2] = load_down(2)
+        w_b = load_words("w_b", EARLY * P, M)
+        u_raw_a = load_rows("u_raw_a", up[:, 0:W])
+        u_raw_b = load_rows("u_raw_b", up[:, W:M])
+        for a in range(PASSES):
+            x_raw[1][a] = load_x(1, a)
+
+        def quantise(name, source, dest_half):
+            grouped = stage.tile([P, W * PACK], BF16, name="grouped", align_bytes=64)
+            codes = keep.tile([P, W], U32, name=name + "_codes", align_bytes=64)
+            scales = keep.tile([P, W], U8, name=name + "_scales", align_bytes=64)
+            nc.vector.tensor_copy(out=dest_half(grouped, 0), in_=source(0))
+            nc.scalar.copy(out=dest_half(grouped, 1), in_=source(1))
+            for s in range(2):
+                nc.vector.quantize_mx(
+                    out=codes[:, s * HALF:(s + 1) * HALF].bitcast(FP8X4),
+                    scales=scales[:, s * HALF:(s + 1) * HALF],
+                    in_=grouped[:, s * HALF * PACK:(s + 1) * HALF * PACK],
+                )
+            return codes, scales
+
+        def plain_half(grouped, s):
+            return grouped[:, s * HALF * PACK:(s + 1) * HALF * PACK].rearrange("p (w j) -> p w j", j=PACK)
+
+        def quantise_rows(name, tile, lo):
+            return quantise(
+                name,
+                lambda s: tile[:, :, lo + s * HALF:lo + (s + 1) * HALF].rearrange("p j w -> p w j"),
+                plain_half,
+            )
+
+        def quantise_down(name, tile):
+            return quantise(
+                name,
+                lambda s: tile[:].rearrange("p j (m t) -> p t m j", t=PACK)[:, 2 * s:2 * s + 2],
+                lambda g, s: g[:, s * HALF * PACK:(s + 1) * HALF * PACK].rearrange("p (t m j) -> p t m j", t=2, j=PACK),
+            )
+
+        x_q = [[None] * PASSES for h in range(T_HALVES)]
+        d_q = [None] * PASSES
+        u_q = [None] * PASSES
+
+        def words(i, a):
+            tile, k = (w_a, i) if i < EARLY else (w_b, i - EARLY)
+            return tile[:, a, 2 * k * P:2 * (k + 1) * P].bitcast(FP4X4)
+
+        def base(acc, h, i, a):
+            nc.tensor.matmul_mx(
+                out=acc[:],
+                lhsT=words(i, a),
+                lhsT_scale=w_scales[:, a, i * P:(i + 1) * P],
+                rhs=x_q[h][a][0][:].bitcast(FP8X4),
+                rhs_scale=x_q[h][a][1][:],
+                start=(a == 0),
+                stop=False,
+            )
+
+        def inner(acc, h, j, a):
+            nc.tensor.matmul_mx(
+                out=acc[:],
+                lhsT=d_q[a][0][:, j * P:(j + 1) * P].bitcast(FP8X4),
+                lhsT_scale=d_q[a][1][:, j * P:(j + 1) * P],
+                rhs=x_q[h][a][0][:].bitcast(FP8X4),
+                rhs_scale=x_q[h][a][1][:],
+                start=(a == 0),
+                stop=(a == PASSES - 1),
+            )
+
+        def bank():
+            acc = psum.tile([P, W], F32, name="acc")
+            return acc
+
+        def evacuate_h(banks):
+            h_raw = stage.tile([P, PACK, W], BF16, name="h_raw", bufs=2)
+            nc.scalar.copy(out=h_raw[:, 0, :], in_=banks[0][:])
+            nc.vector.tensor_copy(out=h_raw[:, 1, :], in_=banks[1][:])
+            nc.scalar.copy(out=h_raw[:, 2, :], in_=banks[2][:])
+            nc.vector.tensor_copy(out=h_raw[:, 3, :], in_=banks[3][:])
+            return h_raw
+
+        state = {"n": 0}
+
+        def close(acc, h, i, h_codes):
+            u = u_q[i // 4]
+            c = (i % 4) * P
+            nc.tensor.matmul_mx(
+                out=acc[:],
+                lhsT=u[0][:, c:c + P].bitcast(FP8X4),
+                lhsT_scale=u[1][:, c:c + P],
+                rhs=h_codes[0][:].bitcast(FP8X4),
+                rhs_scale=h_codes[1][:],
+                start=False,
+                stop=True,
+            )
+            result = outs.tile([P, W], F32, name="result")
+            state["n"] += 1
+            if state["n"] % 3 == 0:
+                nc.vector.tensor_copy(out=result[:], in_=acc[:])
+            else:
+                nc.scalar.copy(out=result[:], in_=acc[:])
+            nc.sync.dma_start(out=out[i * P:(i + 1) * P, h * W:(h + 1) * W], in_=result[:])
+
+        accs = {}
+        h_banks = [bank() for j in range(PACK)]
+        for a in range(PASSES):
+            x_q[0][a] = quantise_rows(f"x_0_{a}", x_raw[0][a], 0)
+            if a > 0:
+                for i in range(EARLY):
+                    base(accs[i], 0, i, a)
+            d_q[a] = quantise_down(f"d_{a}", d_raw[a])
+            for j in range(PACK):
+                inner(h_banks[j], 0, j, a)
+            if a == 0:
+                for i in range(EARLY):
+                    accs[i] = bank()
+                    base(accs[i], 0, i, a)
+        h_raw = evacuate_h(h_banks)
+        for i in range(4, 8):
+            accs[i] = bank()
+            for a in range(PASSES):
+                base(accs[i], 0, i, a)
+        h_q = quantise_rows("h_0", h_raw, 0)
+        u_q[0] = quantise_rows("u_0", u_raw_a, 0)
+        for i in range(4):
+            close(accs[i], 0, i, h_q)
+        u_q[1] = quantise_rows("u_1", u_raw_b, 0)
+
+        def open_tile(h, i):
+            accs[i] = bank()
+            for a in range(PASSES):
+                base(accs[i], h, i, a)
+
+        open_tile(0, 8)
+        open_tile(0, 9)
+        close(accs[4], 0, 4, h_q)
+        close(accs[5], 0, 5, h_q)
+        open_tile(0, 10)
+        u_q[2] = quantise_rows("u_2", u_raw_b, W)
+        close(accs[6], 0, 6, h_q)
+        close(accs[7], 0, 7, h_q)
+        open_tile(0, 11)
+        x_q[1][0] = quantise_rows("x_1_0", x_raw[1][0], 0)
+        for i in range(8, 12):
+            close(accs[i], 0, i, h_q)
+
+        h_banks = [bank() for j in range(PACK)]
+        for i in range(EARLY):
+            accs[i] = bank()
+        for a in range(PASSES):
+            if a > 0:
+                x_q[1][a] = quantise_rows(f"x_1_{a}", x_raw[1][a], 0)
+            for j in range(PACK):
+                inner(h_banks[j], 1, j, a)
+            for i in range(EARLY):
+                base(accs[i], 1, i, a)
+        h_raw = evacuate_h(h_banks)
+        for i in range(4, 7):
+            open_tile(1, i)
+        h_q = quantise_rows("h_1", h_raw, 0)
+        for i in range(7):
+            close(accs[i], 1, i, h_q)
+        for i in range(7, 12):
+            open_tile(1, i)
+            close(accs[i], 1, i, h_q)

@@ -16,11 +16,8 @@ FP4X4 = mybir.dt.float4_e2m1fn_x4
 P = 128
 PACK = 4
 W = 512
-HALF = W // 2
 PASSES = K // W
-N_TILES = M // P
-T_HALVES = T // W
-EARLY = 4
+GROUP = W // P
 
 
 def tile_mix_lowrank_fm_none_kernel(tc, x, w4_words, w4_scales, down, up, out):
@@ -39,201 +36,195 @@ def tile_mix_lowrank_fm_none_kernel(tc, x, w4_words, w4_scales, down, up, out):
         warm_in = keep.tile([P, 8], F32, name="warm_in")
         warm_out = keep.tile([P, 8], F32, name="warm_out")
         nc.vector.memset(warm_in[:], 0.0)
-        nc.scalar.copy(out=warm_out[:], in_=warm_in[:])
 
         def load_rows(name, rows):
             tile = raw.tile([P, PACK, rows.shape[1]], F32, name=name)
             nc.sync.dma_start(out=tile[:], in_=rows.rearrange("(p j) w -> p j w", j=PACK))
             return tile
 
+        x_raw, d_raw, u_raw, w_words = {}, {}, {}, {}
+
         def load_x(h, a):
-            return load_rows(f"x_{h}_{a}", x[a * W:(a + 1) * W, h * W:(h + 1) * W])
+            x_raw[h, a] = load_rows(f"x_{h}_{a}", x[a * W:(a + 1) * W, h * W:(h + 1) * W])
 
         def load_down(a):
-            return load_rows(f"down_{a}", down[a * W:(a + 1) * W, :])
+            d_raw[a] = load_rows(f"down_{a}", down[a * W:(a + 1) * W, :])
 
-        def load_words(name, lo, hi):
-            tile = keep.tile([P, PASSES, 2 * (hi - lo)], U8, name=name, align_bytes=64)
+        def load_up(g):
+            u_raw[g] = load_rows(f"up_{g}", up[:, g * W:(g + 1) * W])
+
+        def load_words(g):
+            w_words[g] = keep.tile([P, PASSES, 2 * W], U8, name=f"w_words_{g}", align_bytes=64)
             nc.sync.dma_start(
-                out=tile[:].bitcast(I32),
-                in_=w4_words[:, :, 2 * lo:2 * hi].rearrange("a p c -> p a c").bitcast(I32),
+                out=w_words[g][:].bitcast(I32),
+                in_=w4_words[:, :, 2 * g * W:2 * (g + 1) * W].rearrange("a p c -> p a c").bitcast(I32),
             )
-            return tile
 
-        x_raw = [[None] * PASSES for h in range(T_HALVES)]
-        d_raw = [None] * PASSES
-        x_raw[0][0] = load_x(0, 0)
-        d_raw[0] = load_down(0)
-        w_a = load_words("w_a", 0, EARLY * P)
+        load_x(0, 0)
+        load_down(0)
+        load_words(0)
         for q in range(4):
             nc.scalar.dma_start(
                 out=w_scales[32 * q:32 * q + 4, :, :].bitcast(I32),
                 in_=w4_scales[:, 4 * q:4 * q + 4, :].rearrange("a r n -> r a n").bitcast(I32),
             )
-        x_raw[0][1] = load_x(0, 1)
-        d_raw[1] = load_down(1)
-        x_raw[0][2] = load_x(0, 2)
-        d_raw[2] = load_down(2)
-        w_b = load_words("w_b", EARLY * P, M)
-        u_raw_a = load_rows("u_raw_a", up[:, 0:W])
-        u_raw_b = load_rows("u_raw_b", up[:, W:M])
+        nc.scalar.copy(out=warm_out[:], in_=warm_in[:])
+        for a in range(1, PASSES):
+            load_x(0, a)
+            load_down(a)
+        load_words(1)
+        load_up(0)
+        load_words(2)
+        load_up(1)
+        load_up(2)
         for a in range(PASSES):
-            x_raw[1][a] = load_x(1, a)
+            load_x(1, a)
 
-        def quantise(name, source, dest_half):
+        def copy_on(engine, dst, src):
+            if engine == "V":
+                nc.vector.tensor_copy(out=dst, in_=src)
+            else:
+                nc.scalar.copy(out=dst, in_=src)
+
+        def quantise(name, view, cuts):
             grouped = stage.tile([P, W * PACK], BF16, name="grouped", align_bytes=64)
             codes = keep.tile([P, W], U32, name=name + "_codes", align_bytes=64)
             scales = keep.tile([P, W], U8, name=name + "_scales", align_bytes=64)
-            nc.vector.tensor_copy(out=dest_half(grouped, 0), in_=source(0))
-            nc.scalar.copy(out=dest_half(grouped, 1), in_=source(1))
-            for s in range(2):
+            for engine, lo, hi in cuts:
+                dst, src = view(grouped, lo, hi)
+                copy_on(engine, dst, src)
+            for lo in (0, W // 2):
+                cols = slice(lo, lo + W // 2)
                 nc.vector.quantize_mx(
-                    out=codes[:, s * HALF:(s + 1) * HALF].bitcast(FP8X4),
-                    scales=scales[:, s * HALF:(s + 1) * HALF],
-                    in_=grouped[:, s * HALF * PACK:(s + 1) * HALF * PACK],
+                    out=codes[:, cols].bitcast(FP8X4),
+                    scales=scales[:, cols],
+                    in_=grouped[:, lo * PACK:(lo + W // 2) * PACK],
                 )
             return codes, scales
 
-        def plain_half(grouped, s):
-            return grouped[:, s * HALF * PACK:(s + 1) * HALF * PACK].rearrange("p (w j) -> p w j", j=PACK)
+        SHARED = (("V",0,256),("S",384,512),("V",256,384))
+        ALONE = (("V", 0, 256), ("V", 256, 512))
 
-        def quantise_rows(name, tile, lo):
-            return quantise(
-                name,
-                lambda s: tile[:, :, lo + s * HALF:lo + (s + 1) * HALF].rearrange("p j w -> p w j"),
-                plain_half,
-            )
+        def quantise_rows(name, tile, cuts):
+            def view(grouped, lo, hi):
+                return (
+                    grouped[:, lo * PACK:hi * PACK].rearrange("p (c i j) -> p c j i", i=4, j=PACK),
+                    tile[:, :, lo:hi].rearrange("p j (c i) -> p c j i", i=4),
+                )
 
-        def quantise_down(name, tile):
-            return quantise(
-                name,
-                lambda s: tile[:].rearrange("p j (m t) -> p t m j", t=PACK)[:, 2 * s:2 * s + 2],
-                lambda g, s: g[:, s * HALF * PACK:(s + 1) * HALF * PACK].rearrange("p (t m j) -> p t m j", t=2, j=PACK),
-            )
+            return quantise(name, view, cuts)
 
-        x_q = [[None] * PASSES for h in range(T_HALVES)]
-        d_q = [None] * PASSES
-        u_q = [None] * PASSES
+        def quantise_down(name, tile, cuts):
+            def view(grouped, lo, hi):
+                return (
+                    grouped[:, lo * PACK:hi * PACK].rearrange("p (t m j) -> p t m j", m=P, j=PACK),
+                    tile[:].rearrange("p j (m t) -> p t m j", t=PACK)[:, lo // P:hi // P],
+                )
 
-        def words(i, a):
-            tile, k = (w_a, i) if i < EARLY else (w_b, i - EARLY)
-            return tile[:, a, 2 * k * P:2 * (k + 1) * P].bitcast(FP4X4)
+            return quantise(name, view, cuts)
 
-        def base(acc, h, i, a):
-            nc.tensor.matmul_mx(
-                out=acc[:],
-                lhsT=words(i, a),
-                lhsT_scale=w_scales[:, a, i * P:(i + 1) * P],
-                rhs=x_q[h][a][0][:].bitcast(FP8X4),
-                rhs_scale=x_q[h][a][1][:],
-                start=(a == 0),
-                stop=False,
-            )
-
-        def inner(acc, h, j, a):
-            nc.tensor.matmul_mx(
-                out=acc[:],
-                lhsT=d_q[a][0][:, j * P:(j + 1) * P].bitcast(FP8X4),
-                lhsT_scale=d_q[a][1][:, j * P:(j + 1) * P],
-                rhs=x_q[h][a][0][:].bitcast(FP8X4),
-                rhs_scale=x_q[h][a][1][:],
-                start=(a == 0),
-                stop=(a == PASSES - 1),
-            )
+        x_q, d_q, u_q, h_q, accs = {}, {}, {}, {}, {}
 
         def bank():
             acc = psum.tile([P, W], F32, name="acc")
             return acc
 
-        def evacuate_h(banks):
-            h_raw = stage.tile([P, PACK, W], BF16, name="h_raw", bufs=2)
-            nc.scalar.copy(out=h_raw[:, 0, :], in_=banks[0][:])
-            nc.vector.tensor_copy(out=h_raw[:, 1, :], in_=banks[1][:])
-            nc.scalar.copy(out=h_raw[:, 2, :], in_=banks[2][:])
-            nc.vector.tensor_copy(out=h_raw[:, 3, :], in_=banks[3][:])
-            return h_raw
-
-        state = {"n": 0}
-
-        def close(acc, h, i, h_codes):
-            u = u_q[i // 4]
-            c = (i % 4) * P
+        def product(acc, lhs, lhs_cols, rhs, start, stop):
             nc.tensor.matmul_mx(
                 out=acc[:],
-                lhsT=u[0][:, c:c + P].bitcast(FP8X4),
-                lhsT_scale=u[1][:, c:c + P],
-                rhs=h_codes[0][:].bitcast(FP8X4),
-                rhs_scale=h_codes[1][:],
-                start=False,
-                stop=True,
+                lhsT=lhs[0][:, lhs_cols].bitcast(FP8X4),
+                lhsT_scale=lhs[1][:, lhs_cols],
+                rhs=rhs[0][:].bitcast(FP8X4),
+                rhs_scale=rhs[1][:],
+                start=start,
+                stop=stop,
             )
-            result = outs.tile([P, W], F32, name="result")
-            state["n"] += 1
-            if state["n"] % 3 == 0:
-                nc.vector.tensor_copy(out=result[:], in_=acc[:])
-            else:
-                nc.scalar.copy(out=result[:], in_=acc[:])
-            nc.sync.dma_start(out=out[i * P:(i + 1) * P, h * W:(h + 1) * W], in_=result[:])
 
-        accs = {}
-        h_banks = [bank() for j in range(PACK)]
-        for a in range(PASSES):
-            x_q[0][a] = quantise_rows(f"x_0_{a}", x_raw[0][a], 0)
-            if a > 0:
-                for i in range(EARLY):
-                    base(accs[i], 0, i, a)
-            d_q[a] = quantise_down(f"d_{a}", d_raw[a])
+        def inner(h, a):
             for j in range(PACK):
-                inner(h_banks[j], 0, j, a)
+                if a == 0:
+                    accs["h", j] = bank()
+                product(accs["h", j], d_q[a], slice(j * P, (j + 1) * P), x_q[h, a], a == 0, a == PASSES - 1)
+
+        def base(h, i, a):
             if a == 0:
-                for i in range(EARLY):
-                    accs[i] = bank()
-                    base(accs[i], 0, i, a)
-        h_raw = evacuate_h(h_banks)
-        for i in range(4, 8):
-            accs[i] = bank()
-            for a in range(PASSES):
-                base(accs[i], 0, i, a)
-        h_q = quantise_rows("h_0", h_raw, 0)
-        u_q[0] = quantise_rows("u_0", u_raw_a, 0)
-        for i in range(4):
-            close(accs[i], 0, i, h_q)
-        u_q[1] = quantise_rows("u_1", u_raw_b, 0)
+                accs[i] = bank()
+            g, k = divmod(i, GROUP)
+            nc.tensor.matmul_mx(
+                out=accs[i][:],
+                lhsT=w_words[g][:, a, 2 * k * P:2 * (k + 1) * P].bitcast(FP4X4),
+                lhsT_scale=w_scales[:, a, i * P:(i + 1) * P],
+                rhs=x_q[h, a][0][:].bitcast(FP8X4),
+                rhs_scale=x_q[h, a][1][:],
+                start=(a == 0),
+                stop=False,
+            )
 
         def open_tile(h, i):
-            accs[i] = bank()
             for a in range(PASSES):
-                base(accs[i], h, i, a)
+                base(h, i, a)
 
+        def empty_inner():
+            h_raw = stage.tile([P, PACK, W], BF16, name="h_raw", bufs=2)
+            for j in range(PACK):
+                copy_on("SV"[j % 2], h_raw[:, j, :], accs["h", j][:])
+            return h_raw
+
+        def close(h, i, engine, parts=1):
+            g, k = divmod(i, GROUP)
+            product(accs[i], u_q[g], slice(k * P, (k + 1) * P), h_q[h], False, True)
+            result = outs.tile([P, W], F32, name="result")
+            for part in range(parts):
+                cols = slice(part * W // parts, (part + 1) * W // parts)
+                copy_on(engine if part % 2 == 0 else "V", result[:, cols], accs[i][:, cols])
+                nc.sync.dma_start(
+                    out=out[i * P:(i + 1) * P, h * W + cols.start:h * W + cols.stop],
+                    in_=result[:, cols],
+                )
+
+        for a in range(PASSES):
+            x_q[0, a] = quantise_rows(f"x_0_{a}", x_raw[0, a], SHARED)
+            if a > 0:
+                for i in range(GROUP):
+                    base(0, i, a)
+            d_q[a] = quantise_down(f"d_{a}", d_raw[a], SHARED)
+            inner(0, a)
+            if a == 0:
+                for i in range(GROUP):
+                    base(0, i, a)
+        h_raw = empty_inner()
+        for i in range(4, 8):
+            open_tile(0, i)
+        h_q[0] = quantise_rows("h_0", h_raw, SHARED)
+        u_q[0] = quantise_rows("u_0", u_raw[0], SHARED)
+        for i in range(4):
+            close(0, i, "S")
         open_tile(0, 8)
         open_tile(0, 9)
-        close(accs[4], 0, 4, h_q)
-        close(accs[5], 0, 5, h_q)
+        u_q[1] = quantise_rows("u_1", u_raw[1], ALONE)
+        close(0, 4, "S")
+        close(0, 5, "S")
         open_tile(0, 10)
-        u_q[2] = quantise_rows("u_2", u_raw_b, W)
-        close(accs[6], 0, 6, h_q)
-        close(accs[7], 0, 7, h_q)
+        close(0, 6, "S")
+        close(0, 7, "S")
         open_tile(0, 11)
-        x_q[1][0] = quantise_rows("x_1_0", x_raw[1][0], 0)
+        u_q[2] = quantise_rows("u_2", u_raw[2], ALONE)
+        x_q[1, 0] = quantise_rows("x_1_0", x_raw[1, 0], ALONE)
         for i in range(8, 12):
-            close(accs[i], 0, i, h_q)
+            close(0, i, "S")
 
-        h_banks = [bank() for j in range(PACK)]
-        for i in range(EARLY):
-            accs[i] = bank()
         for a in range(PASSES):
             if a > 0:
-                x_q[1][a] = quantise_rows(f"x_1_{a}", x_raw[1][a], 0)
-            for j in range(PACK):
-                inner(h_banks[j], 1, j, a)
-            for i in range(EARLY):
-                base(accs[i], 1, i, a)
-        h_raw = evacuate_h(h_banks)
+                x_q[1, a] = quantise_rows(f"x_1_{a}", x_raw[1, a], SHARED)
+            inner(1, a)
+            for i in range(GROUP):
+                base(1, i, a)
+        h_raw = empty_inner()
         for i in range(4, 7):
             open_tile(1, i)
-        h_q = quantise_rows("h_1", h_raw, 0)
+        h_q[1] = quantise_rows("h_1", h_raw, SHARED)
         for i in range(7):
-            close(accs[i], 1, i, h_q)
+            close(1, i, "SV"[i % 2])
         for i in range(7, 12):
             open_tile(1, i)
-            close(accs[i], 1, i, h_q)
+            close(1, i, "SV"[i % 2], parts=2 if i == 11 else 1)

@@ -117,8 +117,8 @@ def tile_mix_lowrank_fm_none_kernel(tc, x, w4_words, w4_scales, down, up, out):
         def quantise_down(name, tile, cuts):
             def view(grouped, lo, hi):
                 return (
-                    grouped[:, lo * PACK:hi * PACK].rearrange("p (t m j) -> p t m j", m=P, j=PACK),
-                    tile[:].rearrange("p j (m t) -> p t m j", t=PACK)[:, lo // P:hi // P],
+                    grouped[:].rearrange("p (t m j) -> p m j t", t=PACK, j=PACK)[:, lo // PACK:hi // PACK],
+                    tile[:].rearrange("p j (m t) -> p m j t", t=PACK)[:, lo // PACK:hi // PACK],
                 )
 
             return quantise(name, view, cuts)
@@ -220,11 +220,11 @@ def tile_mix_lowrank_fm_none_kernel(tc, x, w4_words, w4_scales, down, up, out):
             for i in range(GROUP):
                 base(1, i, a)
         h_raw = empty_inner()
-        for i in range(4, 7):
+        for i in range(4, 6):
             open_tile(1, i)
         h_q[1] = quantise_rows("h_1", h_raw, SHARED)
-        for i in range(7):
+        for i in range(6):
             close(1, i, "SV"[i % 2])
-        for i in range(7, 12):
+        for i in range(6, 12):
             open_tile(1, i)
             close(1, i, "SV"[i % 2], parts=2 if i == 11 else 1)

from contextlib import ExitStack

import concourse.mybir as mybir

K, R, M, T = 1536, 512, 1536, 1024
FLOPS = 2 * T * (K * R + K * M + R * M)

F32 = mybir.dt.float32
BF16 = mybir.dt.bfloat16
U32 = mybir.dt.uint32
I32 = mybir.dt.int32
U8 = mybir.dt.uint8
FP8X4 = mybir.dt.float8_e4m3fn_x4
FP4X4 = mybir.dt.float4_e2m1fn_x4

P = 128
PACK = 4
W = 512
PASSES = K // W
GROUP = W // P


def tile_mix_lowrank_fm_none_kernel(tc, x, w4_words, w4_scales, down, up, out):
    nc = tc.nc

    with ExitStack() as ctx:
        raw = ctx.enter_context(tc.tile_pool(name="raw", bufs=1))
        stage = ctx.enter_context(tc.tile_pool(name="stage", bufs=4))
        keep = ctx.enter_context(tc.tile_pool(name="keep", bufs=1))
        outs = ctx.enter_context(tc.tile_pool(name="outs", bufs=24))
        psum = ctx.enter_context(tc.psum_pool(name="psum", bufs=8))
        ctx.enter_context(tc.manual_schedule())

        w_scales = keep.tile([P, PASSES, M], U8, name="w_scales", align_bytes=64)
        nc.vector.memset(w_scales[:].rearrange("p a n -> p (a n)").bitcast(I32), 0)
        warm_in = keep.tile([P, 8], F32, name="warm_in")
        warm_out = keep.tile([P, 8], F32, name="warm_out")
        nc.vector.memset(warm_in[:], 0.0)

        def load_rows(name, rows):
            tile = raw.tile([P, PACK, rows.shape[1]], F32, name=name)
            nc.sync.dma_start(out=tile[:], in_=rows.rearrange("(p j) w -> p j w", j=PACK))
            return tile

        x_raw, d_raw, u_raw, w_words = {}, {}, {}, {}

        def load_x(h, a):
            x_raw[h, a] = load_rows(f"x_{h}_{a}", x[a * W:(a + 1) * W, h * W:(h + 1) * W])

        def load_down(a):
            d_raw[a] = load_rows(f"down_{a}", down[a * W:(a + 1) * W, :])

        def load_up(g):
            u_raw[g] = load_rows(f"up_{g}", up[:, g * W:(g + 1) * W])

        def load_words(g):
            w_words[g] = keep.tile([P, PASSES, 2 * W], U8, name=f"w_words_{g}", align_bytes=64)
            nc.sync.dma_start(
                out=w_words[g][:].bitcast(I32),
                in_=w4_words[:, :, 2 * g * W:2 * (g + 1) * W].rearrange("a p c -> p a c").bitcast(I32),
            )

        load_x(0, 0)
        load_down(0)
        load_words(0)
        for q in range(4):
            nc.scalar.dma_start(
                out=w_scales[32 * q:32 * q + 4, :, :].bitcast(I32),
                in_=w4_scales[:, 4 * q:4 * q + 4, :].rearrange("a r n -> r a n").bitcast(I32),
            )
        nc.scalar.copy(out=warm_out[:], in_=warm_in[:])
        for a in range(1, PASSES):
            load_x(0, a)
            load_down(a)
        load_words(1)
        load_up(0)
        load_words(2)
        load_up(1)
        load_up(2)
        for a in range(PASSES):
            load_x(1, a)

        def copy_on(engine, dst, src):
            if engine == "V":
                nc.vector.tensor_copy(out=dst, in_=src)
            else:
                nc.scalar.copy(out=dst, in_=src)

        def quantise(name, view, cuts):
            grouped = stage.tile([P, W * PACK], BF16, name="grouped", align_bytes=64)
            codes = keep.tile([P, W], U32, name=name + "_codes", align_bytes=64)
            scales = keep.tile([P, W], U8, name=name + "_scales", align_bytes=64)
            for engine, lo, hi in cuts:
                dst, src = view(grouped, lo, hi)
                copy_on(engine, dst, src)
            for lo in (0, W // 2):
                cols = slice(lo, lo + W // 2)
                nc.vector.quantize_mx(
                    out=codes[:, cols].bitcast(FP8X4),
                    scales=scales[:, cols],
                    in_=grouped[:, lo * PACK:(lo + W // 2) * PACK],
                )
            return codes, scales

        SHARED = (("V",0,256),("S",384,512),("V",256,384))
        ALONE = (("V", 0, 256), ("V", 256, 512))

        def quantise_rows(name, tile, cuts):
            def view(grouped, lo, hi):
                return (
                    grouped[:, lo * PACK:hi * PACK].rearrange("p (c i j) -> p c j i", i=4, j=PACK),
                    tile[:, :, lo:hi].rearrange("p j (c i) -> p c j i", i=4),
                )

            return quantise(name, view, cuts)

        def quantise_down(name, tile, cuts):
            def view(grouped, lo, hi):
                return (
                    grouped[:].rearrange("p (t m j) -> p m j t", t=PACK, j=PACK)[:, lo // PACK:hi // PACK],
                    tile[:].rearrange("p j (m t) -> p m j t", t=PACK)[:, lo // PACK:hi // PACK],
                )

            return quantise(name, view, cuts)

        x_q, d_q, u_q, h_q, accs = {}, {}, {}, {}, {}

        def bank():
            acc = psum.tile([P, W], F32, name="acc")
            return acc

        def product(acc, lhs, lhs_cols, rhs, start, stop):
            nc.tensor.matmul_mx(
                out=acc[:],
                lhsT=lhs[0][:, lhs_cols].bitcast(FP8X4),
                lhsT_scale=lhs[1][:, lhs_cols],
                rhs=rhs[0][:].bitcast(FP8X4),
                rhs_scale=rhs[1][:],
                start=start,
                stop=stop,
            )

        def inner(h, a):
            for j in range(PACK):
                if a == 0:
                    accs["h", j] = bank()
                product(accs["h", j], d_q[a], slice(j * P, (j + 1) * P), x_q[h, a], a == 0, a == PASSES - 1)

        def base(h, i, a):
            if a == 0:
                accs[i] = bank()
            g, k = divmod(i, GROUP)
            nc.tensor.matmul_mx(
                out=accs[i][:],
                lhsT=w_words[g][:, a, 2 * k * P:2 * (k + 1) * P].bitcast(FP4X4),
                lhsT_scale=w_scales[:, a, i * P:(i + 1) * P],
                rhs=x_q[h, a][0][:].bitcast(FP8X4),
                rhs_scale=x_q[h, a][1][:],
                start=(a == 0),
                stop=False,
            )

        def open_tile(h, i):
            for a in range(PASSES):
                base(h, i, a)

        def empty_inner():
            h_raw = stage.tile([P, PACK, W], BF16, name="h_raw", bufs=2)
            for j in range(PACK):
                copy_on("SV"[j % 2], h_raw[:, j, :], accs["h", j][:])
            return h_raw

        def close(h, i, engine, parts=1):
            g, k = divmod(i, GROUP)
            product(accs[i], u_q[g], slice(k * P, (k + 1) * P), h_q[h], False, True)
            result = outs.tile([P, W], F32, name="result")
            for part in range(parts):
                cols = slice(part * W // parts, (part + 1) * W // parts)
                copy_on(engine if part % 2 == 0 else "V", result[:, cols], accs[i][:, cols])
                nc.sync.dma_start(
                    out=out[i * P:(i + 1) * P, h * W + cols.start:h * W + cols.stop],
                    in_=result[:, cols],
                )

        for a in range(PASSES):
            x_q[0, a] = quantise_rows(f"x_0_{a}", x_raw[0, a], SHARED)
            if a > 0:
                for i in range(GROUP):
                    base(0, i, a)
            d_q[a] = quantise_down(f"d_{a}", d_raw[a], SHARED)
            inner(0, a)
            if a == 0:
                for i in range(GROUP):
                    base(0, i, a)
        h_raw = empty_inner()
        for i in range(4, 8):
            open_tile(0, i)
        h_q[0] = quantise_rows("h_0", h_raw, SHARED)
        u_q[0] = quantise_rows("u_0", u_raw[0], SHARED)
        for i in range(4):
            close(0, i, "S")
        open_tile(0, 8)
        open_tile(0, 9)
        u_q[1] = quantise_rows("u_1", u_raw[1], ALONE)
        close(0, 4, "S")
        close(0, 5, "S")
        open_tile(0, 10)
        close(0, 6, "S")
        close(0, 7, "S")
        open_tile(0, 11)
        u_q[2] = quantise_rows("u_2", u_raw[2], ALONE)
        x_q[1, 0] = quantise_rows("x_1_0", x_raw[1, 0], ALONE)
        for i in range(8, 12):
            close(0, i, "S")

        for a in range(PASSES):
            if a > 0:
                x_q[1, a] = quantise_rows(f"x_1_{a}", x_raw[1, a], SHARED)
            inner(1, a)
            for i in range(GROUP):
                base(1, i, a)
        h_raw = empty_inner()
        for i in range(4, 6):
            open_tile(1, i)
        h_q[1] = quantise_rows("h_1", h_raw, SHARED)
        for i in range(6):
            close(1, i, "SV"[i % 2])
        for i in range(6, 12):
            open_tile(1, i)
            close(1, i, "SV"[i % 2], parts=2 if i == 11 else 1)
